import numpy as np
import ml_dtypes


def mxq(x, axis, fmt="e4m3"):
    dtype, down = {"e4m3": (ml_dtypes.float8_e4m3fn, 7), "e5m2": (ml_dtypes.float8_e5m2, 14)}[fmt]
    v = np.moveaxis(np.asarray(x, np.float32).astype(ml_dtypes.bfloat16).astype(np.float64), axis, -1)
    blocks = v.reshape(v.shape[:-1] + (-1, 32))
    amax = np.abs(blocks).max(-1, keepdims=True)
    byte = np.maximum(np.where(amax > 0, np.frexp(amax)[1] - 1 + 127, 0) - down, 1)
    scale = np.exp2(byte - 127.0)
    codes = (blocks / scale).astype(np.float32).astype(dtype).astype(np.float64)
    return np.moveaxis((codes * scale).reshape(v.shape), -1, axis)


WIDE = False


def mx_kscale(k):
    if not WIDE:
        return np.ones(k)
    levels = np.array([10, -10, 5, -5, 0])
    if k % 512:
        return np.exp2(np.random.permutation(np.resize(levels, k // 32))).repeat(32)
    a = np.empty((k // 512, 16))
    for p in range(k // 512):
        a[p, :8] = np.random.permutation(np.resize(levels, 8))
        for g in range(8):
            far = levels[np.abs(levels - a[p, g]) >= 10]
            a[p, g + 8] = far[np.random.randint(len(far))]
    return np.exp2(a.ravel()).repeat(32)


def f64(x):
    return np.asarray(x).astype(np.float64)


def striped(idx):
    return np.tile(idx.reshape(-1, 16).T, (8, 1)).astype(np.uint16)


def unstriped(offs):
    return offs[:16].T.reshape(-1).astype(np.int64)


K, T, E, C, N = 1024, 2048, 8, 128, 128


def by_expert(wq, xq):
    return np.concatenate([wq[e].T @ xq[:, e * C:(e + 1) * C] for e in range(E)], axis=1)


def setup_inputs():
    n = np.random.standard_normal
    s = mx_kscale(K)[:, None]
    return {
        "xT": (n((K, T)) * s).astype(np.float32),
        "w": (n((E, K, N)) / np.sqrt(K) / s[None]).astype(np.float32),
        "gate": np.tile(np.random.uniform(0.2, 1.0, E * C), (N, 1)).astype(np.float32),
        "offs": striped(np.random.permutation(T)[:E * C]),
    }


def reference(xT, w, gate, offs):
    idx = unstriped(offs)
    xq = mxq(f64(xT)[:, idx], 0, "e4m3")
    y = by_expert(mxq(f64(w), 1, "e4m3"), xq)
    out = np.zeros((N, T))
    out[:, idx] = f64(gate) * y
    return out

@@ -1,0 +1,154 @@
+import concourse.mybir as mybir
+
+FLOPS = 2 * 1024 * 128 * 1024
+
+K, T, E, C, N = 1024, 2048, 8, 128, 128
+P = 128
+PACK = 4
+PASSES = K // (P * PACK)
+SLOTS = E * C
+
+F32 = mybir.dt.float32
+BF16 = mybir.dt.bfloat16
+U32 = mybir.dt.uint32
+U16 = mybir.dt.uint16
+U8 = mybir.dt.uint8
+FP8X4 = mybir.dt.float8_e4m3fn_x4
+MULT = mybir.AluOpType.mult
+
+HALF = 512
+QUARTER = 256
+
+
+def tile_routed_moe_kernel(tc, xT, w, gate, offs, out):
+    nc = tc.nc
+    planes_hbm = xT.rearrange("(g p t) n -> g p t n", p=P, t=PACK)
+    w_hbm = w.flatten_outer_dims().rearrange("(c p t) n -> p c (t n)", p=P, t=PACK)
+
+    with tc.tile_pool(name="keep", bufs=1) as keep, tc.psum_pool(name="psum", bufs=1) as psum:
+        offs_sb = keep.tile([P, SLOTS // 16], U16, name="offs_sb")
+        nc.sync.dma_start(offs_sb[:], offs)
+
+        plane = [[keep.tile([P, T], F32, name="plane%d_%d" % (g, t)) for t in range(PACK)] for g in range(PASSES)]
+        w_raw = [keep.tile([P, 4, PACK * N], F32, name="w_raw%d" % j) for j in range(4)]
+        gate_sb = keep.tile([P, SLOTS], F32, name="gate_sb")
+
+        def load_plane(g, t):
+            nc.sync.dma_start(plane[g][t][:], planes_hbm[g, :, t, :])
+
+        def load_w(j):
+            nc.sync.dma_start(w_raw[j][:], w_hbm[:, 4 * j : 4 * j + 4, :])
+
+        for t in range(PACK):
+            load_plane(0, t)
+        load_plane(1, 0)
+        load_plane(1, 1)
+        load_w(0)
+        load_plane(1, 2)
+        load_w(1)
+        load_plane(1, 3)
+        load_w(2)
+        nc.sync.dma_start(gate_sb[:], gate)
+        load_w(3)
+
+        window = keep.tile([P, T], F32, name="window")
+        nc.vector.memset(window[:], 0.0)
+
+        g4 = [[keep.tile([P, PACK, HALF], F32, name="g4_%d_%d" % (g, h)) for h in range(2)] for g in range(PASSES)]
+        tokg0 = keep.tile([P, SLOTS, PACK], BF16, name="tokg0", align_bytes=64)
+        tokg1 = [keep.tile([P, QUARTER, PACK], BF16, name="tokg1_%d" % q, align_bytes=64) for q in range(4)]
+        tok_codes = [keep.tile([P, SLOTS], U32, name="tok_codes%d" % g, align_bytes=64) for g in range(PASSES)]
+        tok_scales = [keep.tile([P, SLOTS], U8, name="tok_scales%d" % g, align_bytes=64) for g in range(PASSES)]
+        w_grouped = [keep.tile([P, 4, N, PACK], BF16, name="w_grouped%d" % j, align_bytes=64) for j in range(4)]
+        w_codes = keep.tile([P, 16 * N], U32, name="w_codes", align_bytes=64)
+        w_scales = keep.tile([P, 16 * N], U8, name="w_scales", align_bytes=64)
+
+        def gather(g, t, first, count):
+            h, a = first // HALF, first % HALF
+            nc.vector.tensor_copy(
+                g4[g][h][:, t, a : a + count],
+                plane[g][t][:].indirect(offs_sb[:, first // 16 : (first + count) // 16]),
+            )
+
+        def interleave_tokens0(h):
+            nc.scalar.copy(tokg0[:, h * HALF : (h + 1) * HALF, :], g4[0][h][:].rearrange("p t n -> p n t"))
+
+        def interleave_tokens1(q):
+            h, a = q // 2, (q % 2) * QUARTER
+            src = g4[1][h][:, :, a : a + QUARTER].rearrange("p t n -> p n t")
+            if q == 3:
+                nc.vector.tensor_copy(tokg1[q][:], src)
+            else:
+                nc.scalar.copy(tokg1[q][:], src)
+
+        def quantize_tokens1(q):
+            cols = slice(q * QUARTER, (q + 1) * QUARTER)
+            nc.vector.quantize_mx(
+                out=tok_codes[1][:, cols].bitcast(FP8X4),
+                scales=tok_scales[1][:, cols],
+                in_=tokg1[q][:].rearrange("p n t -> p (n t)"),
+            )
+
+        def interleave_w(j):
+            for c in range(0, 4, 2):
+                nc.scalar.copy(
+                    w_grouped[j][:, c : c + 2, :, :],
+                    w_raw[j][:, c : c + 2, :].rearrange("p c (t n) -> p c n t", t=PACK),
+                )
+
+        def quantize_w(j):
+            cols = slice(j * 4 * N, (j + 1) * 4 * N)
+            nc.vector.quantize_mx(
+                out=w_codes[:, cols].bitcast(FP8X4),
+                scales=w_scales[:, cols],
+                in_=w_grouped[j][:].rearrange("p c n t -> p (c n t)"),
+            )
+
+        for t in range(PACK):
+            for h in range(2):
+                gather(0, t, h * HALF, HALF)
+                if t == PACK - 1:
+                    interleave_tokens0(h)
+        interleave_w(0)
+        interleave_w(1)
+        for t in range(PACK - 1):
+            for h in range(2):
+                gather(1, t, h * HALF, HALF)
+        for q in range(4):
+            gather(1, PACK - 1, q * QUARTER, QUARTER)
+            interleave_tokens1(q)
+
+        nc.vector.quantize_mx(
+            out=tok_codes[0][:].bitcast(FP8X4),
+            scales=tok_scales[0][:],
+            in_=tokg0[:].rearrange("p n t -> p (n t)"),
+        )
+        for j in range(4):
+            if j >= 2:
+                interleave_w(j)
+            quantize_w(j)
+            quantize_tokens1(j)
+            acc = psum.tile([P, QUARTER], F32, name="acc%d" % j)
+            for e in (2 * j, 2 * j + 1):
+                for g in range(PASSES):
+                    wc = slice((2 * e + g) * N, (2 * e + g + 1) * N)
+                    sc = slice(e * C, (e + 1) * C)
+                    nc.tensor.matmul_mx(
+                        out=acc[:, (e % 2) * C : (e % 2 + 1) * C],
+                        lhsT=w_codes[:, wc].bitcast(FP8X4),
+                        lhsT_scale=w_scales[:, wc],
+                        rhs=tok_codes[g][:, sc].bitcast(FP8X4),
+                        rhs_scale=tok_scales[g][:, sc],
+                        start=(g == 0),
+                        stop=(g == PASSES - 1),
+                    )
+            sums = keep.tile([P, QUARTER], F32, name="sums%d" % j)
+            nc.scalar.copy(sums[:], acc[:])
+            nc.vector.tensor_tensor(
+                window[:].indirect(offs_sb[:, j * QUARTER // 16 : (j + 1) * QUARTER // 16]),
+                sums[:],
+                gate_sb[:, j * QUARTER : (j + 1) * QUARTER],
+                MULT,
+            )
+
+        nc.sync.dma_start(out, window[:])

@@ -29,12 +29,12 @@ def tile_routed_moe_kernel(tc, xT, w, gate, offs, out):
         offs_sb = keep.tile([P, SLOTS // 16], U16, name="offs_sb")
         nc.sync.dma_start(offs_sb[:], offs)
 
-        plane = [[keep.tile([P, T], F32, name="plane%d_%d" % (g, t)) for t in range(PACK)] for g in range(PASSES)]
+        raw = [keep.tile([P, PACK, T], F32, name="raw%d" % g) for g in range(PASSES)]
         w_raw = [keep.tile([P, 4, PACK * N], F32, name="w_raw%d" % j) for j in range(4)]
         gate_sb = keep.tile([P, SLOTS], F32, name="gate_sb")
 
         def load_plane(g, t):
-            nc.sync.dma_start(plane[g][t][:], planes_hbm[g, :, t, :])
+            nc.sync.dma_start(raw[g][:, t, :], planes_hbm[g, :, t, :])
 
         def load_w(j):
             nc.sync.dma_start(w_raw[j][:], w_hbm[:, 4 * j : 4 * j + 4, :])
@@ -54,9 +54,7 @@ def tile_routed_moe_kernel(tc, xT, w, gate, offs, out):
         window = keep.tile([P, T], F32, name="window")
         nc.vector.memset(window[:], 0.0)
 
-        g4 = [[keep.tile([P, PACK, HALF], F32, name="g4_%d_%d" % (g, h)) for h in range(2)] for g in range(PASSES)]
-        tokg0 = keep.tile([P, SLOTS, PACK], BF16, name="tokg0", align_bytes=64)
-        tokg1 = [keep.tile([P, QUARTER, PACK], BF16, name="tokg1_%d" % q, align_bytes=64) for q in range(4)]
+        tokg = [keep.tile([P, SLOTS, PACK], BF16, name="tokg%d" % g, align_bytes=64) for g in range(PASSES)]
         tok_codes = [keep.tile([P, SLOTS], U32, name="tok_codes%d" % g, align_bytes=64) for g in range(PASSES)]
         tok_scales = [keep.tile([P, SLOTS], U8, name="tok_scales%d" % g, align_bytes=64) for g in range(PASSES)]
         w_grouped = [keep.tile([P, 4, N, PACK], BF16, name="w_grouped%d" % j, align_bytes=64) for j in range(4)]
@@ -64,29 +62,17 @@ def tile_routed_moe_kernel(tc, xT, w, gate, offs, out):
         w_scales = keep.tile([P, 16 * N], U8, name="w_scales", align_bytes=64)
 
         def gather(g, t, first, count):
-            h, a = first // HALF, first % HALF
             nc.vector.tensor_copy(
-                g4[g][h][:, t, a : a + count],
-                plane[g][t][:].indirect(offs_sb[:, first // 16 : (first + count) // 16]),
+                tokg[g][:, first : first + count, t],
+                raw[g][:, t, :].indirect(offs_sb[:, first // 16 : (first + count) // 16]),
             )
 
-        def interleave_tokens0(h):
-            nc.scalar.copy(tokg0[:, h * HALF : (h + 1) * HALF, :], g4[0][h][:].rearrange("p t n -> p n t"))
-
-        def interleave_tokens1(q):
-            h, a = q // 2, (q % 2) * QUARTER
-            src = g4[1][h][:, :, a : a + QUARTER].rearrange("p t n -> p n t")
-            if q == 3:
-                nc.vector.tensor_copy(tokg1[q][:], src)
-            else:
-                nc.scalar.copy(tokg1[q][:], src)
-
-        def quantize_tokens1(q):
-            cols = slice(q * QUARTER, (q + 1) * QUARTER)
+        def quantize_tokens(g, first, count):
+            cols = slice(first, first + count)
             nc.vector.quantize_mx(
-                out=tok_codes[1][:, cols].bitcast(FP8X4),
-                scales=tok_scales[1][:, cols],
-                in_=tokg1[q][:].rearrange("p n t -> p (n t)"),
+                out=tok_codes[g][:, cols].bitcast(FP8X4),
+                scales=tok_scales[g][:, cols],
+                in_=tokg[g][:, cols, :].rearrange("p n t -> p (n t)"),
             )
 
         def interleave_w(j):
@@ -107,27 +93,17 @@ def tile_routed_moe_kernel(tc, xT, w, gate, offs, out):
         for t in range(PACK):
             for h in range(2):
                 gather(0, t, h * HALF, HALF)
-                if t == PACK - 1:
-                    interleave_tokens0(h)
-        interleave_w(0)
-        interleave_w(1)
         for t in range(PACK - 1):
             for h in range(2):
                 gather(1, t, h * HALF, HALF)
         for q in range(4):
             gather(1, PACK - 1, q * QUARTER, QUARTER)
-            interleave_tokens1(q)
 
-        nc.vector.quantize_mx(
-            out=tok_codes[0][:].bitcast(FP8X4),
-            scales=tok_scales[0][:],
-            in_=tokg0[:].rearrange("p n t -> p (n t)"),
-        )
+        quantize_tokens(0, 0, SLOTS)
         for j in range(4):
-            if j >= 2:
-                interleave_w(j)
+            interleave_w(j)
             quantize_w(j)
-            quantize_tokens1(j)
+            quantize_tokens(1, j * QUARTER, QUARTER)
             acc = psum.tile([P, QUARTER], F32, name="acc%d" % j)
             for e in (2 * j, 2 * j + 1):
                 for g in range(PASSES):

@@ -29,12 +29,12 @@ def tile_routed_moe_kernel(tc, xT, w, gate, offs, out):
         offs_sb = keep.tile([P, SLOTS // 16], U16, name="offs_sb")
         nc.sync.dma_start(offs_sb[:], offs)
 
-        raw = [keep.tile([P, PACK, T], F32, name="raw%d" % g) for g in range(PASSES)]
+        plane = [[keep.tile([P, T], F32, name="plane%d_%d" % (g, t)) for t in range(PACK)] for g in range(PASSES)]
         w_raw = [keep.tile([P, 4, PACK * N], F32, name="w_raw%d" % j) for j in range(4)]
         gate_sb = keep.tile([P, SLOTS], F32, name="gate_sb")
 
         def load_plane(g, t):
-            nc.sync.dma_start(raw[g][:, t, :], planes_hbm[g, :, t, :])
+            nc.sync.dma_start(plane[g][t][:], planes_hbm[g, :, t, :])
 
         def load_w(j):
             nc.sync.dma_start(w_raw[j][:], w_hbm[:, 4 * j : 4 * j + 4, :])
@@ -54,7 +54,9 @@ def tile_routed_moe_kernel(tc, xT, w, gate, offs, out):
         window = keep.tile([P, T], F32, name="window")
         nc.vector.memset(window[:], 0.0)
 
-        tokg = [keep.tile([P, SLOTS, PACK], BF16, name="tokg%d" % g, align_bytes=64) for g in range(PASSES)]
+        g4 = [[keep.tile([P, PACK, HALF], F32, name="g4_%d_%d" % (g, h)) for h in range(2)] for g in range(PASSES)]
+        tokg0 = keep.tile([P, SLOTS, PACK], BF16, name="tokg0", align_bytes=64)
+        tokg1 = [keep.tile([P, QUARTER, PACK], BF16, name="tokg1_%d" % q, align_bytes=64) for q in range(4)]
         tok_codes = [keep.tile([P, SLOTS], U32, name="tok_codes%d" % g, align_bytes=64) for g in range(PASSES)]
         tok_scales = [keep.tile([P, SLOTS], U8, name="tok_scales%d" % g, align_bytes=64) for g in range(PASSES)]
         w_grouped = [keep.tile([P, 4, N, PACK], BF16, name="w_grouped%d" % j, align_bytes=64) for j in range(4)]
@@ -62,24 +64,40 @@ def tile_routed_moe_kernel(tc, xT, w, gate, offs, out):
         w_scales = keep.tile([P, 16 * N], U8, name="w_scales", align_bytes=64)
 
         def gather(g, t, first, count):
+            h, a = first // HALF, first % HALF
             nc.vector.tensor_copy(
-                tokg[g][:, first : first + count, t],
-                raw[g][:, t, :].indirect(offs_sb[:, first // 16 : (first + count) // 16]),
+                g4[g][h][:, t, a : a + count],
+                plane[g][t][:].indirect(offs_sb[:, first // 16 : (first + count) // 16]),
             )
 
-        def quantize_tokens(g, first, count):
-            cols = slice(first, first + count)
+        def interleave_tokens0(h):
+            nc.scalar.copy(
+                tokg0[:, h * HALF : (h + 1) * HALF, :].rearrange("p (c i) t -> p c t i", i=4),
+                g4[0][h][:].rearrange("p t (c i) -> p c t i", i=4),
+            )
+
+        def interleave_tokens1(q):
+            h, a = q // 2, (q % 2) * QUARTER
+            src = g4[1][h][:, :, a : a + QUARTER].rearrange("p t (c i) -> p c t i", i=4)
+            dst = tokg1[q][:].rearrange("p (c i) t -> p c t i", i=4)
+            if q == 3:
+                nc.vector.tensor_copy(dst, src)
+            else:
+                nc.scalar.copy(dst, src)
+
+        def quantize_tokens1(q):
+            cols = slice(q * QUARTER, (q + 1) * QUARTER)
             nc.vector.quantize_mx(
-                out=tok_codes[g][:, cols].bitcast(FP8X4),
-                scales=tok_scales[g][:, cols],
-                in_=tokg[g][:, cols, :].rearrange("p n t -> p (n t)"),
+                out=tok_codes[1][:, cols].bitcast(FP8X4),
+                scales=tok_scales[1][:, cols],
+                in_=tokg1[q][:].rearrange("p n t -> p (n t)"),
             )
 
         def interleave_w(j):
             for c in range(0, 4, 2):
                 nc.scalar.copy(
-                    w_grouped[j][:, c : c + 2, :, :],
-                    w_raw[j][:, c : c + 2, :].rearrange("p c (t n) -> p c n t", t=PACK),
+                    w_grouped[j][:, c : c + 2, :, :].rearrange("p c (b i) t -> p c b t i", i=4),
+                    w_raw[j][:, c : c + 2, :].rearrange("p c (t b i) -> p c b t i", t=PACK, i=4),
                 )
 
         def quantize_w(j):
@@ -93,17 +111,27 @@ def tile_routed_moe_kernel(tc, xT, w, gate, offs, out):
         for t in range(PACK):
             for h in range(2):
                 gather(0, t, h * HALF, HALF)
+                if t == PACK - 1:
+                    interleave_tokens0(h)
+        interleave_w(0)
+        interleave_w(1)
         for t in range(PACK - 1):
             for h in range(2):
                 gather(1, t, h * HALF, HALF)
         for q in range(4):
             gather(1, PACK - 1, q * QUARTER, QUARTER)
+            interleave_tokens1(q)
 
-        quantize_tokens(0, 0, SLOTS)
+        nc.vector.quantize_mx(
+            out=tok_codes[0][:].bitcast(FP8X4),
+            scales=tok_scales[0][:],
+            in_=tokg0[:].rearrange("p n t -> p (n t)"),
+        )
         for j in range(4):
-            interleave_w(j)
+            if j >= 2:
+                interleave_w(j)
             quantize_w(j)
-            quantize_tokens(1, j * QUARTER, QUARTER)
+            quantize_tokens1(j)
             acc = psum.tile([P, QUARTER], F32, name="acc%d" % j)
             for e in (2 * j, 2 * j + 1):
                 for g in range(PASSES):

@@ -15,9 +15,14 @@ U16 = mybir.dt.uint16
 U8 = mybir.dt.uint8
 FP8X4 = mybir.dt.float8_e4m3fn_x4
 MULT = mybir.AluOpType.mult
+COPY = mybir.ActivationFunctionType.Copy
 
 HALF = 512
 QUARTER = 256
+LOADS = ["p0","p1","p2","p3","p4","p5","p6","w0","p7","gate","w1","w2","w3"]
+VECTOR_W = ((1, 2), (2, 2), (3, 2))
+VECTOR_T1 = (3,)
+SCALAR_CAST = ()
 
 
 def tile_routed_moe_kernel(tc, xT, w, gate, offs, out):
@@ -33,28 +38,22 @@ def tile_routed_moe_kernel(tc, xT, w, gate, offs, out):
         w_raw = [keep.tile([P, 4, PACK * N], F32, name="w_raw%d" % j) for j in range(4)]
         gate_sb = keep.tile([P, SLOTS], F32, name="gate_sb")
 
-        def load_plane(g, t):
-            nc.sync.dma_start(plane[g][t][:], planes_hbm[g, :, t, :])
-
-        def load_w(j):
-            nc.sync.dma_start(w_raw[j][:], w_hbm[:, 4 * j : 4 * j + 4, :])
-
-        for t in range(PACK):
-            load_plane(0, t)
-        load_plane(1, 0)
-        load_plane(1, 1)
-        load_w(0)
-        load_plane(1, 2)
-        load_w(1)
-        load_plane(1, 3)
-        load_w(2)
-        nc.sync.dma_start(gate_sb[:], gate)
-        load_w(3)
+        for item in LOADS:
+            if item[0] == "p":
+                k = int(item[1])
+                nc.sync.dma_start(plane[k // PACK][k % PACK][:], planes_hbm[k // PACK, :, k % PACK, :])
+            elif item[0] == "w":
+                j = int(item[1])
+                nc.sync.dma_start(w_raw[j][:], w_hbm[:, 4 * j : 4 * j + 4, :])
+            else:
+                nc.sync.dma_start(gate_sb[:], gate)
 
         window = keep.tile([P, T], F32, name="window")
         nc.vector.memset(window[:], 0.0)
 
-        g4 = [[keep.tile([P, PACK, HALF], F32, name="g4_%d_%d" % (g, h)) for h in range(2)] for g in range(PASSES)]
+        xb = keep.tile([P, 2, T], BF16, name="xb")
+        g2 = [keep.tile([P, 2, HALF], F32, name="g2_%d" % h) for h in range(2)]
+        g4 = [keep.tile([P, PACK, HALF], F32, name="g4_%d" % h) for h in range(2)]
         tokg0 = keep.tile([P, SLOTS, PACK], BF16, name="tokg0", align_bytes=64)
         tokg1 = [keep.tile([P, QUARTER, PACK], BF16, name="tokg1_%d" % q, align_bytes=64) for q in range(4)]
         tok_codes = [keep.tile([P, SLOTS], U32, name="tok_codes%d" % g, align_bytes=64) for g in range(PASSES)]
@@ -62,25 +61,16 @@ def tile_routed_moe_kernel(tc, xT, w, gate, offs, out):
         w_grouped = [keep.tile([P, 4, N, PACK], BF16, name="w_grouped%d" % j, align_bytes=64) for j in range(4)]
         w_codes = keep.tile([P, 16 * N], U32, name="w_codes", align_bytes=64)
         w_scales = keep.tile([P, 16 * N], U8, name="w_scales", align_bytes=64)
+        sums = [keep.tile([P, QUARTER], F32, name="sums%d" % j) for j in range(4)]
 
-        def gather(g, t, first, count):
-            h, a = first // HALF, first % HALF
-            nc.vector.tensor_copy(
-                g4[g][h][:, t, a : a + count],
-                plane[g][t][:].indirect(offs_sb[:, first // 16 : (first + count) // 16]),
-            )
-
-        def interleave_tokens0(h):
-            nc.scalar.copy(
-                tokg0[:, h * HALF : (h + 1) * HALF, :].rearrange("p (c i) t -> p c t i", i=4),
-                g4[0][h][:].rearrange("p t (c i) -> p c t i", i=4),
-            )
+        def offsets(first, count):
+            return offs_sb[:, first // 16 : (first + count) // 16]
 
         def interleave_tokens1(q):
             h, a = q // 2, (q % 2) * QUARTER
-            src = g4[1][h][:, :, a : a + QUARTER].rearrange("p t (c i) -> p c t i", i=4)
+            src = g4[h][:, :, a : a + QUARTER].rearrange("p t (c i) -> p c t i", i=4)
             dst = tokg1[q][:].rearrange("p (c i) t -> p c t i", i=4)
-            if q == 3:
+            if q in VECTOR_T1:
                 nc.vector.tensor_copy(dst, src)
             else:
                 nc.scalar.copy(dst, src)
@@ -95,10 +85,12 @@ def tile_routed_moe_kernel(tc, xT, w, gate, offs, out):
 
         def interleave_w(j):
             for c in range(0, 4, 2):
-                nc.scalar.copy(
-                    w_grouped[j][:, c : c + 2, :, :].rearrange("p c (b i) t -> p c b t i", i=4),
-                    w_raw[j][:, c : c + 2, :].rearrange("p c (t b i) -> p c b t i", t=PACK, i=4),
-                )
+                dst = w_grouped[j][:, c : c + 2, :, :].rearrange("p c (b i) t -> p c b t i", i=4)
+                src = w_raw[j][:, c : c + 2, :].rearrange("p c (t b i) -> p c b t i", t=PACK, i=4)
+                if (j, c) in VECTOR_W:
+                    nc.vector.tensor_copy(dst, src)
+                else:
+                    nc.scalar.copy(dst, src)
 
         def quantize_w(j):
             cols = slice(j * 4 * N, (j + 1) * 4 * N)
@@ -108,18 +100,35 @@ def tile_routed_moe_kernel(tc, xT, w, gate, offs, out):
                 in_=w_grouped[j][:].rearrange("p c n t -> p (c n t)"),
             )
 
-        for t in range(PACK):
+        for t in range(2):
+            if t in SCALAR_CAST:
+                nc.scalar.copy(xb[:, t, :], plane[0][t][:])
+            else:
+                nc.vector.tensor_copy(xb[:, t, :], plane[0][t][:])
             for h in range(2):
-                gather(0, t, h * HALF, HALF)
+                nc.scalar.activation(
+                    tokg0[:, h * HALF : (h + 1) * HALF, t],
+                    xb[:, t, :].indirect(offsets(h * HALF, HALF)),
+                    COPY,
+                )
+        for t in range(2, PACK):
+            for h in range(2):
+                nc.vector.tensor_copy(g2[h][:, t - 2, :], plane[0][t][:].indirect(offsets(h * HALF, HALF)))
                 if t == PACK - 1:
-                    interleave_tokens0(h)
-        interleave_w(0)
-        interleave_w(1)
+                    nc.scalar.copy(
+                        tokg0[:, h * HALF : (h + 1) * HALF, 2:PACK],
+                        g2[h][:].rearrange("p t n -> p n t"),
+                    )
+        for j in range(1):
+            interleave_w(j)
         for t in range(PACK - 1):
             for h in range(2):
-                gather(1, t, h * HALF, HALF)
+                nc.vector.tensor_copy(g4[h][:, t, :], plane[1][t][:].indirect(offsets(h * HALF, HALF)))
         for q in range(4):
-            gather(1, PACK - 1, q * QUARTER, QUARTER)
+            h, a = q // 2, (q % 2) * QUARTER
+            nc.vector.tensor_copy(
+                g4[h][:, PACK - 1, a : a + QUARTER], plane[1][PACK - 1][:].indirect(offsets(q * QUARTER, QUARTER))
+            )
             interleave_tokens1(q)
 
         nc.vector.quantize_mx(
@@ -128,7 +137,7 @@ def tile_routed_moe_kernel(tc, xT, w, gate, offs, out):
             in_=tokg0[:].rearrange("p n t -> p (n t)"),
         )
         for j in range(4):
-            if j >= 2:
+            if j >= 1:
                 interleave_w(j)
             quantize_w(j)
             quantize_tokens1(j)
@@ -146,11 +155,10 @@ def tile_routed_moe_kernel(tc, xT, w, gate, offs, out):
                         start=(g == 0),
                         stop=(g == PASSES - 1),
                     )
-            sums = keep.tile([P, QUARTER], F32, name="sums%d" % j)
-            nc.scalar.copy(sums[:], acc[:])
+            nc.scalar.copy(sums[j][:], acc[:])
             nc.vector.tensor_tensor(
-                window[:].indirect(offs_sb[:, j * QUARTER // 16 : (j + 1) * QUARTER // 16]),
-                sums[:],
+                window[:].indirect(offsets(j * QUARTER, QUARTER)),
+                sums[j][:],
                 gate_sb[:, j * QUARTER : (j + 1) * QUARTER],
                 MULT,
             )

@@ -15,14 +15,9 @@ U16 = mybir.dt.uint16
 U8 = mybir.dt.uint8
 FP8X4 = mybir.dt.float8_e4m3fn_x4
 MULT = mybir.AluOpType.mult
-COPY = mybir.ActivationFunctionType.Copy
 
 HALF = 512
 QUARTER = 256
-LOADS = ["p0","p1","p2","p3","p4","p5","p6","w0","p7","gate","w1","w2","w3"]
-VECTOR_W = ((1, 2), (2, 2), (3, 2))
-VECTOR_T1 = (3,)
-SCALAR_CAST = ()
 
 
 def tile_routed_moe_kernel(tc, xT, w, gate, offs, out):
@@ -38,22 +33,28 @@ def tile_routed_moe_kernel(tc, xT, w, gate, offs, out):
         w_raw = [keep.tile([P, 4, PACK * N], F32, name="w_raw%d" % j) for j in range(4)]
         gate_sb = keep.tile([P, SLOTS], F32, name="gate_sb")
 
-        for item in LOADS:
-            if item[0] == "p":
-                k = int(item[1])
-                nc.sync.dma_start(plane[k // PACK][k % PACK][:], planes_hbm[k // PACK, :, k % PACK, :])
-            elif item[0] == "w":
-                j = int(item[1])
-                nc.sync.dma_start(w_raw[j][:], w_hbm[:, 4 * j : 4 * j + 4, :])
-            else:
-                nc.sync.dma_start(gate_sb[:], gate)
+        def load_plane(g, t):
+            nc.sync.dma_start(plane[g][t][:], planes_hbm[g, :, t, :])
+
+        def load_w(j):
+            nc.sync.dma_start(w_raw[j][:], w_hbm[:, 4 * j : 4 * j + 4, :])
+
+        for t in range(PACK):
+            load_plane(0, t)
+        load_plane(1, 0)
+        load_plane(1, 1)
+        load_w(0)
+        load_plane(1, 2)
+        load_w(1)
+        load_plane(1, 3)
+        load_w(2)
+        nc.sync.dma_start(gate_sb[:], gate)
+        load_w(3)
 
         window = keep.tile([P, T], F32, name="window")
         nc.vector.memset(window[:], 0.0)
 
-        xb = keep.tile([P, 2, T], BF16, name="xb")
-        g2 = [keep.tile([P, 2, HALF], F32, name="g2_%d" % h) for h in range(2)]
-        g4 = [keep.tile([P, PACK, HALF], F32, name="g4_%d" % h) for h in range(2)]
+        g4 = [[keep.tile([P, PACK, HALF], F32, name="g4_%d_%d" % (g, h)) for h in range(2)] for g in range(PASSES)]
         tokg0 = keep.tile([P, SLOTS, PACK], BF16, name="tokg0", align_bytes=64)
         tokg1 = [keep.tile([P, QUARTER, PACK], BF16, name="tokg1_%d" % q, align_bytes=64) for q in range(4)]
         tok_codes = [keep.tile([P, SLOTS], U32, name="tok_codes%d" % g, align_bytes=64) for g in range(PASSES)]
@@ -61,16 +62,25 @@ def tile_routed_moe_kernel(tc, xT, w, gate, offs, out):
         w_grouped = [keep.tile([P, 4, N, PACK], BF16, name="w_grouped%d" % j, align_bytes=64) for j in range(4)]
         w_codes = keep.tile([P, 16 * N], U32, name="w_codes", align_bytes=64)
         w_scales = keep.tile([P, 16 * N], U8, name="w_scales", align_bytes=64)
-        sums = [keep.tile([P, QUARTER], F32, name="sums%d" % j) for j in range(4)]
 
-        def offsets(first, count):
-            return offs_sb[:, first // 16 : (first + count) // 16]
+        def gather(g, t, first, count):
+            h, a = first // HALF, first % HALF
+            nc.vector.tensor_copy(
+                g4[g][h][:, t, a : a + count],
+                plane[g][t][:].indirect(offs_sb[:, first // 16 : (first + count) // 16]),
+            )
+
+        def interleave_tokens0(h):
+            nc.scalar.copy(
+                tokg0[:, h * HALF : (h + 1) * HALF, :].rearrange("p (c i) t -> p c t i", i=4),
+                g4[0][h][:].rearrange("p t (c i) -> p c t i", i=4),
+            )
 
         def interleave_tokens1(q):
             h, a = q // 2, (q % 2) * QUARTER
-            src = g4[h][:, :, a : a + QUARTER].rearrange("p t (c i) -> p c t i", i=4)
+            src = g4[1][h][:, :, a : a + QUARTER].rearrange("p t (c i) -> p c t i", i=4)
             dst = tokg1[q][:].rearrange("p (c i) t -> p c t i", i=4)
-            if q in VECTOR_T1:
+            if q == 3:
                 nc.vector.tensor_copy(dst, src)
             else:
                 nc.scalar.copy(dst, src)
@@ -85,12 +95,10 @@ def tile_routed_moe_kernel(tc, xT, w, gate, offs, out):
 
         def interleave_w(j):
             for c in range(0, 4, 2):
-                dst = w_grouped[j][:, c : c + 2, :, :].rearrange("p c (b i) t -> p c b t i", i=4)
-                src = w_raw[j][:, c : c + 2, :].rearrange("p c (t b i) -> p c b t i", t=PACK, i=4)
-                if (j, c) in VECTOR_W:
-                    nc.vector.tensor_copy(dst, src)
-                else:
-                    nc.scalar.copy(dst, src)
+                nc.scalar.copy(
+                    w_grouped[j][:, c : c + 2, :, :].rearrange("p c (b i) t -> p c b t i", i=4),
+                    w_raw[j][:, c : c + 2, :].rearrange("p c (t b i) -> p c b t i", t=PACK, i=4),
+                )
 
         def quantize_w(j):
             cols = slice(j * 4 * N, (j + 1) * 4 * N)
@@ -100,35 +108,18 @@ def tile_routed_moe_kernel(tc, xT, w, gate, offs, out):
                 in_=w_grouped[j][:].rearrange("p c n t -> p (c n t)"),
             )
 
-        for t in range(2):
-            if t in SCALAR_CAST:
-                nc.scalar.copy(xb[:, t, :], plane[0][t][:])
-            else:
-                nc.vector.tensor_copy(xb[:, t, :], plane[0][t][:])
+        for t in range(PACK):
             for h in range(2):
-                nc.scalar.activation(
-                    tokg0[:, h * HALF : (h + 1) * HALF, t],
-                    xb[:, t, :].indirect(offsets(h * HALF, HALF)),
-                    COPY,
-                )
-        for t in range(2, PACK):
-            for h in range(2):
-                nc.vector.tensor_copy(g2[h][:, t - 2, :], plane[0][t][:].indirect(offsets(h * HALF, HALF)))
+                gather(0, t, h * HALF, HALF)
                 if t == PACK - 1:
-                    nc.scalar.copy(
-                        tokg0[:, h * HALF : (h + 1) * HALF, 2:PACK],
-                        g2[h][:].rearrange("p t n -> p n t"),
-                    )
-        for j in range(1):
-            interleave_w(j)
+                    interleave_tokens0(h)
+        interleave_w(0)
+        interleave_w(1)
         for t in range(PACK - 1):
             for h in range(2):
-                nc.vector.tensor_copy(g4[h][:, t, :], plane[1][t][:].indirect(offsets(h * HALF, HALF)))
+                gather(1, t, h * HALF, HALF)
         for q in range(4):
-            h, a = q // 2, (q % 2) * QUARTER
-            nc.vector.tensor_copy(
-                g4[h][:, PACK - 1, a : a + QUARTER], plane[1][PACK - 1][:].indirect(offsets(q * QUARTER, QUARTER))
-            )
+            gather(1, PACK - 1, q * QUARTER, QUARTER)
             interleave_tokens1(q)
 
         nc.vector.quantize_mx(
@@ -136,30 +127,38 @@ def tile_routed_moe_kernel(tc, xT, w, gate, offs, out):
             scales=tok_scales[0][:],
             in_=tokg0[:].rearrange("p n t -> p (n t)"),
         )
+        sums = keep.tile([P, SLOTS], F32, name="sums")
+        acc = [psum.tile([P, C], F32, name="acc%d" % e) for e in range(E)]
+
+        def multiply(e, g):
+            wc = slice((2 * e + g) * N, (2 * e + g + 1) * N)
+            sc = slice(e * C, (e + 1) * C)
+            nc.tensor.matmul_mx(
+                out=acc[e][:],
+                lhsT=w_codes[:, wc].bitcast(FP8X4),
+                lhsT_scale=w_scales[:, wc],
+                rhs=tok_codes[g][:, sc].bitcast(FP8X4),
+                rhs_scale=tok_scales[g][:, sc],
+                start=(g == 0),
+                stop=(g == PASSES - 1),
+            )
+
         for j in range(4):
-            if j >= 1:
+            if j >= 2:
                 interleave_w(j)
             quantize_w(j)
+            multiply(2 * j, 0)
+            multiply(2 * j + 1, 0)
             quantize_tokens1(j)
-            acc = psum.tile([P, QUARTER], F32, name="acc%d" % j)
             for e in (2 * j, 2 * j + 1):
-                for g in range(PASSES):
-                    wc = slice((2 * e + g) * N, (2 * e + g + 1) * N)
-                    sc = slice(e * C, (e + 1) * C)
-                    nc.tensor.matmul_mx(
-                        out=acc[:, (e % 2) * C : (e % 2 + 1) * C],
-                        lhsT=w_codes[:, wc].bitcast(FP8X4),
-                        lhsT_scale=w_scales[:, wc],
-                        rhs=tok_codes[g][:, sc].bitcast(FP8X4),
-                        rhs_scale=tok_scales[g][:, sc],
-                        start=(g == 0),
-                        stop=(g == PASSES - 1),
-                    )
-            nc.scalar.copy(sums[j][:], acc[:])
+                multiply(e, 1)
+                nc.scalar.copy(sums[:, e * C : (e + 1) * C], acc[e][:])
+
+        for first, count in ((0, HALF), (HALF, QUARTER), (HALF + QUARTER, QUARTER)):
             nc.vector.tensor_tensor(
-                window[:].indirect(offsets(j * QUARTER, QUARTER)),
-                sums[j][:],
-                gate_sb[:, j * QUARTER : (j + 1) * QUARTER],
+                window[:].indirect(offs_sb[:, first // 16 : (first + count) // 16]),
+                sums[:, first : first + count],
+                gate_sb[:, first : first + count],
                 MULT,
             )
 

@@ -54,7 +54,7 @@ def tile_routed_moe_kernel(tc, xT, w, gate, offs, out):
         window = keep.tile([P, T], F32, name="window")
         nc.vector.memset(window[:], 0.0)
 
-        g4 = [[keep.tile([P, PACK, HALF], F32, name="g4_%d_%d" % (g, h)) for h in range(2)] for g in range(PASSES)]
+        g4 = [keep.tile([P, PACK, SLOTS], F32, name="g4_%d" % g) for g in range(PASSES)]
         tokg0 = keep.tile([P, SLOTS, PACK], BF16, name="tokg0", align_bytes=64)
         tokg1 = [keep.tile([P, QUARTER, PACK], BF16, name="tokg1_%d" % q, align_bytes=64) for q in range(4)]
         tok_codes = [keep.tile([P, SLOTS], U32, name="tok_codes%d" % g, align_bytes=64) for g in range(PASSES)]
@@ -64,21 +64,19 @@ def tile_routed_moe_kernel(tc, xT, w, gate, offs, out):
         w_scales = keep.tile([P, 16 * N], U8, name="w_scales", align_bytes=64)
 
         def gather(g, t, first, count):
-            h, a = first // HALF, first % HALF
             nc.vector.tensor_copy(
-                g4[g][h][:, t, a : a + count],
+                g4[g][:, t, first : first + count],
                 plane[g][t][:].indirect(offs_sb[:, first // 16 : (first + count) // 16]),
             )
 
         def interleave_tokens0(h):
             nc.scalar.copy(
                 tokg0[:, h * HALF : (h + 1) * HALF, :].rearrange("p (c i) t -> p c t i", i=4),
-                g4[0][h][:].rearrange("p t (c i) -> p c t i", i=4),
+                g4[0][:, :, h * HALF : (h + 1) * HALF].rearrange("p t (c i) -> p c t i", i=4),
             )
 
         def interleave_tokens1(q):
-            h, a = q // 2, (q % 2) * QUARTER
-            src = g4[1][h][:, :, a : a + QUARTER].rearrange("p t (c i) -> p c t i", i=4)
+            src = g4[1][:, :, q * QUARTER : (q + 1) * QUARTER].rearrange("p t (c i) -> p c t i", i=4)
             dst = tokg1[q][:].rearrange("p (c i) t -> p c t i", i=4)
             if q == 3:
                 nc.vector.tensor_copy(dst, src)
@@ -109,15 +107,13 @@ def tile_routed_moe_kernel(tc, xT, w, gate, offs, out):
             )
 
         for t in range(PACK):
-            for h in range(2):
-                gather(0, t, h * HALF, HALF)
-                if t == PACK - 1:
-                    interleave_tokens0(h)
+            gather(0, t, 0, SLOTS)
+        for h in range(2):
+            interleave_tokens0(h)
         interleave_w(0)
         interleave_w(1)
         for t in range(PACK - 1):
-            for h in range(2):
-                gather(1, t, h * HALF, HALF)
+            gather(1, t, 0, SLOTS)
         for q in range(4):
             gather(1, PACK - 1, q * QUARTER, QUARTER)
             interleave_tokens1(q)

@@ -15,9 +15,12 @@ U16 = mybir.dt.uint16
 U8 = mybir.dt.uint8
 FP8X4 = mybir.dt.float8_e4m3fn_x4
 MULT = mybir.AluOpType.mult
+COPY = mybir.ActivationFunctionType.Copy
 
-HALF = 512
 QUARTER = 256
+
+W_ON_VECTOR = (3,)
+TOKENS_ON_VECTOR = (2, 3)
 
 
 def tile_routed_moe_kernel(tc, xT, w, gate, offs, out):
@@ -33,28 +36,18 @@ def tile_routed_moe_kernel(tc, xT, w, gate, offs, out):
         w_raw = [keep.tile([P, 4, PACK * N], F32, name="w_raw%d" % j) for j in range(4)]
         gate_sb = keep.tile([P, SLOTS], F32, name="gate_sb")
 
-        def load_plane(g, t):
-            nc.sync.dma_start(plane[g][t][:], planes_hbm[g, :, t, :])
-
-        def load_w(j):
-            nc.sync.dma_start(w_raw[j][:], w_hbm[:, 4 * j : 4 * j + 4, :])
-
         for t in range(PACK):
-            load_plane(0, t)
-        load_plane(1, 0)
-        load_plane(1, 1)
-        load_w(0)
-        load_plane(1, 2)
-        load_w(1)
-        load_plane(1, 3)
-        load_w(2)
+            for g in range(PASSES):
+                nc.sync.dma_start(plane[g][t][:], planes_hbm[g, :, t, :])
         nc.sync.dma_start(gate_sb[:], gate)
-        load_w(3)
+        for j in range(4):
+            nc.sync.dma_start(w_raw[j][:], w_hbm[:, 4 * j : 4 * j + 4, :])
 
         window = keep.tile([P, T], F32, name="window")
         nc.vector.memset(window[:], 0.0)
 
-        g4 = [keep.tile([P, PACK, SLOTS], F32, name="g4_%d" % g) for g in range(PASSES)]
+        plane16 = [keep.tile([P, T], BF16, name="plane16_%d" % t) for t in range(PACK)]
+        g4 = keep.tile([P, PACK, SLOTS], F32, name="g4")
         tokg0 = keep.tile([P, SLOTS, PACK], BF16, name="tokg0", align_bytes=64)
         tokg1 = [keep.tile([P, QUARTER, PACK], BF16, name="tokg1_%d" % q, align_bytes=64) for q in range(4)]
         tok_codes = [keep.tile([P, SLOTS], U32, name="tok_codes%d" % g, align_bytes=64) for g in range(PASSES)]
@@ -63,22 +56,16 @@ def tile_routed_moe_kernel(tc, xT, w, gate, offs, out):
         w_codes = keep.tile([P, 16 * N], U32, name="w_codes", align_bytes=64)
         w_scales = keep.tile([P, 16 * N], U8, name="w_scales", align_bytes=64)
 
-        def gather(g, t, first, count):
-            nc.vector.tensor_copy(
-                g4[g][:, t, first : first + count],
-                plane[g][t][:].indirect(offs_sb[:, first // 16 : (first + count) // 16]),
-            )
+        def listed(first, count):
+            return offs_sb[:, first // 16 : (first + count) // 16]
 
-        def interleave_tokens0(h):
-            nc.scalar.copy(
-                tokg0[:, h * HALF : (h + 1) * HALF, :].rearrange("p (c i) t -> p c t i", i=4),
-                g4[0][:, :, h * HALF : (h + 1) * HALF].rearrange("p t (c i) -> p c t i", i=4),
-            )
+        def gather(t, first, count):
+            nc.vector.tensor_copy(g4[:, t, first : first + count], plane[1][t][:].indirect(listed(first, count)))
 
         def interleave_tokens1(q):
-            src = g4[1][:, :, q * QUARTER : (q + 1) * QUARTER].rearrange("p t (c i) -> p c t i", i=4)
+            src = g4[:, :, q * QUARTER : (q + 1) * QUARTER].rearrange("p t (c i) -> p c t i", i=4)
             dst = tokg1[q][:].rearrange("p (c i) t -> p c t i", i=4)
-            if q == 3:
+            if q in TOKENS_ON_VECTOR:
                 nc.vector.tensor_copy(dst, src)
             else:
                 nc.scalar.copy(dst, src)
@@ -91,12 +78,14 @@ def tile_routed_moe_kernel(tc, xT, w, gate, offs, out):
                 in_=tokg1[q][:].rearrange("p n t -> p (n t)"),
             )
 
-        def interleave_w(j):
-            for c in range(0, 4, 2):
-                nc.scalar.copy(
-                    w_grouped[j][:, c : c + 2, :, :].rearrange("p c (b i) t -> p c b t i", i=4),
-                    w_raw[j][:, c : c + 2, :].rearrange("p c (t b i) -> p c b t i", t=PACK, i=4),
-                )
+        def interleave_expert(e):
+            j, c = e // 2, 2 * (e % 2)
+            dst = w_grouped[j][:, c : c + 2, :, :].rearrange("p c (b i) t -> p c b t i", i=4)
+            src = w_raw[j][:, c : c + 2, :].rearrange("p c (t b i) -> p c b t i", t=PACK, i=4)
+            if e in W_ON_VECTOR:
+                nc.vector.tensor_copy(dst, src)
+            else:
+                nc.scalar.copy(dst, src)
 
         def quantize_w(j):
             cols = slice(j * 4 * N, (j + 1) * 4 * N)
@@ -107,15 +96,14 @@ def tile_routed_moe_kernel(tc, xT, w, gate, offs, out):
             )
 
         for t in range(PACK):
-            gather(0, t, 0, SLOTS)
-        for h in range(2):
-            interleave_tokens0(h)
-        interleave_w(0)
-        interleave_w(1)
-        for t in range(PACK - 1):
-            gather(1, t, 0, SLOTS)
+            nc.vector.tensor_copy(plane16[t][:], plane[0][t][:])
+            nc.scalar.activation(tokg0[:, :, t], plane16[t][:].indirect(listed(0, SLOTS)), COPY)
+            if t < PACK - 1:
+                gather(t, 0, SLOTS)
+            else:
+                for q in range(4):
+                    gather(t, q * QUARTER, QUARTER)
         for q in range(4):
-            gather(1, PACK - 1, q * QUARTER, QUARTER)
             interleave_tokens1(q)
 
         nc.vector.quantize_mx(
@@ -123,6 +111,9 @@ def tile_routed_moe_kernel(tc, xT, w, gate, offs, out):
             scales=tok_scales[0][:],
             in_=tokg0[:].rearrange("p n t -> p (n t)"),
         )
+        for q in range(4):
+            quantize_tokens1(q)
+
         sums = keep.tile([P, SLOTS], F32, name="sums")
         acc = [psum.tile([P, C], F32, name="acc%d" % e) for e in range(E)]
 
@@ -139,22 +130,24 @@ def tile_routed_moe_kernel(tc, xT, w, gate, offs, out):
                 stop=(g == PASSES - 1),
             )
 
+        interleave_expert(0)
+        interleave_expert(1)
         for j in range(4):
-            if j >= 2:
-                interleave_w(j)
+            if j < 3:
+                interleave_expert(2 * j + 2)
+                interleave_expert(2 * j + 3)
             quantize_w(j)
             multiply(2 * j, 0)
             multiply(2 * j + 1, 0)
-            quantize_tokens1(j)
             for e in (2 * j, 2 * j + 1):
                 multiply(e, 1)
                 nc.scalar.copy(sums[:, e * C : (e + 1) * C], acc[e][:])
 
-        for first, count in ((0, HALF), (HALF, QUARTER), (HALF + QUARTER, QUARTER)):
+        for first in range(0, SLOTS, QUARTER):
             nc.vector.tensor_tensor(
-                window[:].indirect(offs_sb[:, first // 16 : (first + count) // 16]),
-                sums[:, first : first + count],
-                gate_sb[:, first : first + count],
+                window[:].indirect(listed(first, QUARTER)),
+                sums[:, first : first + QUARTER],
+                gate_sb[:, first : first + QUARTER],
                 MULT,
             )
 

@@ -17,6 +17,7 @@ FP8X4 = mybir.dt.float8_e4m3fn_x4
 MULT = mybir.AluOpType.mult
 COPY = mybir.ActivationFunctionType.Copy
 
+HALF = 512
 QUARTER = 256
 
 W_ON_VECTOR = (3,)
@@ -33,7 +34,7 @@ def tile_routed_moe_kernel(tc, xT, w, gate, offs, out):
         nc.sync.dma_start(offs_sb[:], offs)
 
         plane = [[keep.tile([P, T], F32, name="plane%d_%d" % (g, t)) for t in range(PACK)] for g in range(PASSES)]
-        w_raw = [keep.tile([P, 4, PACK * N], F32, name="w_raw%d" % j) for j in range(4)]
+        w_raw = [keep.tile([P, 4, PACK * N], F32, name="w_raw%d" % j, tag="w_raw%d" % j) for j in range(4)]
         gate_sb = keep.tile([P, SLOTS], F32, name="gate_sb")
 
         for t in range(PACK):
@@ -49,7 +50,7 @@ def tile_routed_moe_kernel(tc, xT, w, gate, offs, out):
         plane16 = [keep.tile([P, T], BF16, name="plane16_%d" % t) for t in range(PACK)]
         g4 = keep.tile([P, PACK, SLOTS], F32, name="g4")
         tokg0 = keep.tile([P, SLOTS, PACK], BF16, name="tokg0", align_bytes=64)
-        tokg1 = [keep.tile([P, QUARTER, PACK], BF16, name="tokg1_%d" % q, align_bytes=64) for q in range(4)]
+        tokg1 = [keep.tile([P, HALF, PACK], BF16, name="tokg1_%d" % h, align_bytes=64) for h in range(2)]
         tok_codes = [keep.tile([P, SLOTS], U32, name="tok_codes%d" % g, align_bytes=64) for g in range(PASSES)]
         tok_scales = [keep.tile([P, SLOTS], U8, name="tok_scales%d" % g, align_bytes=64) for g in range(PASSES)]
         w_grouped = [keep.tile([P, 4, N, PACK], BF16, name="w_grouped%d" % j, align_bytes=64) for j in range(4)]
@@ -64,18 +65,19 @@ def tile_routed_moe_kernel(tc, xT, w, gate, offs, out):
 
         def interleave_tokens1(q):
             src = g4[:, :, q * QUARTER : (q + 1) * QUARTER].rearrange("p t (c i) -> p c t i", i=4)
-            dst = tokg1[q][:].rearrange("p (c i) t -> p c t i", i=4)
+            a = (q % 2) * QUARTER
+            dst = tokg1[q // 2][:, a : a + QUARTER, :].rearrange("p (c i) t -> p c t i", i=4)
             if q in TOKENS_ON_VECTOR:
                 nc.vector.tensor_copy(dst, src)
             else:
                 nc.scalar.copy(dst, src)
 
-        def quantize_tokens1(q):
-            cols = slice(q * QUARTER, (q + 1) * QUARTER)
+        def quantize_tokens1(h):
+            cols = slice(h * HALF, (h + 1) * HALF)
             nc.vector.quantize_mx(
                 out=tok_codes[1][:, cols].bitcast(FP8X4),
                 scales=tok_scales[1][:, cols],
-                in_=tokg1[q][:].rearrange("p n t -> p (n t)"),
+                in_=tokg1[h][:].rearrange("p n t -> p (n t)"),
             )
 
         def interleave_expert(e):
@@ -101,8 +103,8 @@ def tile_routed_moe_kernel(tc, xT, w, gate, offs, out):
             if t < PACK - 1:
                 gather(t, 0, SLOTS)
             else:
-                for q in range(4):
-                    gather(t, q * QUARTER, QUARTER)
+                for h in range(2):
+                    gather(t, h * HALF, HALF)
         for q in range(4):
             interleave_tokens1(q)
 
@@ -111,10 +113,10 @@ def tile_routed_moe_kernel(tc, xT, w, gate, offs, out):
             scales=tok_scales[0][:],
             in_=tokg0[:].rearrange("p n t -> p (n t)"),
         )
-        for q in range(4):
-            quantize_tokens1(q)
+        for h in range(2):
+            quantize_tokens1(h)
 
-        sums = keep.tile([P, SLOTS], F32, name="sums")
+        sums = []
         acc = [psum.tile([P, C], F32, name="acc%d" % e) for e in range(E)]
 
         def multiply(e, g):
@@ -139,14 +141,16 @@ def tile_routed_moe_kernel(tc, xT, w, gate, offs, out):
             quantize_w(j)
             multiply(2 * j, 0)
             multiply(2 * j + 1, 0)
+            sums.append(keep.tile([P, 2 * C], F32, name="sums%d" % j, tag=("w_raw%d" % (j + 1)) if j < 3 else "sums3"))
             for e in (2 * j, 2 * j + 1):
                 multiply(e, 1)
-                nc.scalar.copy(sums[:, e * C : (e + 1) * C], acc[e][:])
+                nc.scalar.copy(sums[j][:, (e % 2) * C : (e % 2 + 1) * C], acc[e][:])
 
-        for first in range(0, SLOTS, QUARTER):
+        for j in range(4):
+            first = j * QUARTER
             nc.vector.tensor_tensor(
                 window[:].indirect(listed(first, QUARTER)),
-                sums[:, first : first + QUARTER],
+                sums[j][:],
                 gate_sb[:, first : first + QUARTER],
                 MULT,
             )

@@ -22,6 +22,7 @@ QUARTER = 256
 
 W_ON_VECTOR = (3,)
 TOKENS_ON_VECTOR = (2, 3)
+PLANE_ORDER = ((0, 0), (0, 1), (1, 0), (0, 2), (1, 1), (0, 3), (1, 2), (1, 3))
 
 
 def tile_routed_moe_kernel(tc, xT, w, gate, offs, out):
@@ -37,9 +38,8 @@ def tile_routed_moe_kernel(tc, xT, w, gate, offs, out):
         w_raw = [keep.tile([P, 4, PACK * N], F32, name="w_raw%d" % j, tag="w_raw%d" % j) for j in range(4)]
         gate_sb = keep.tile([P, SLOTS], F32, name="gate_sb")
 
-        for t in range(PACK):
-            for g in range(PASSES):
-                nc.sync.dma_start(plane[g][t][:], planes_hbm[g, :, t, :])
+        for g, t in PLANE_ORDER:
+            nc.sync.dma_start(plane[g][t][:], planes_hbm[g, :, t, :])
         nc.sync.dma_start(gate_sb[:], gate)
         for j in range(4):
             nc.sync.dma_start(w_raw[j][:], w_hbm[:, 4 * j : 4 * j + 4, :])
@@ -97,10 +97,11 @@ def tile_routed_moe_kernel(tc, xT, w, gate, offs, out):
                 in_=w_grouped[j][:].rearrange("p c n t -> p (c n t)"),
             )
 
-        for t in range(PACK):
-            nc.vector.tensor_copy(plane16[t][:], plane[0][t][:])
-            nc.scalar.activation(tokg0[:, :, t], plane16[t][:].indirect(listed(0, SLOTS)), COPY)
-            if t < PACK - 1:
+        for g, t in PLANE_ORDER:
+            if g == 0:
+                nc.vector.tensor_copy(plane16[t][:], plane[0][t][:])
+                nc.scalar.activation(tokg0[:, :, t], plane16[t][:].indirect(listed(0, SLOTS)), COPY)
+            elif t < PACK - 1:
                 gather(t, 0, SLOTS)
             else:
                 for h in range(2):

@@ -21,7 +21,7 @@ HALF = 512
 QUARTER = 256
 
 W_ON_VECTOR = (3,)
-TOKENS_ON_VECTOR = (2, 3)
+TOKENS_ON_VECTOR = (1,)
 PLANE_ORDER = ((0, 0), (0, 1), (1, 0), (0, 2), (1, 1), (0, 3), (1, 2), (1, 3))
 
 
@@ -34,7 +34,7 @@ def tile_routed_moe_kernel(tc, xT, w, gate, offs, out):
         offs_sb = keep.tile([P, SLOTS // 16], U16, name="offs_sb")
         nc.sync.dma_start(offs_sb[:], offs)
 
-        plane = [[keep.tile([P, T], F32, name="plane%d_%d" % (g, t)) for t in range(PACK)] for g in range(PASSES)]
+        plane = [[keep.tile([P, T], F32, name="plane%d_%d" % (g, t), tag="plane%d_%d" % (g, t), align_bytes=64) for t in range(PACK)] for g in range(PASSES)]
         w_raw = [keep.tile([P, 4, PACK * N], F32, name="w_raw%d" % j, tag="w_raw%d" % j) for j in range(4)]
         gate_sb = keep.tile([P, SLOTS], F32, name="gate_sb")
 
@@ -50,8 +50,8 @@ def tile_routed_moe_kernel(tc, xT, w, gate, offs, out):
         plane16 = [keep.tile([P, T], BF16, name="plane16_%d" % t) for t in range(PACK)]
         g4 = keep.tile([P, PACK, SLOTS], F32, name="g4")
         tokg0 = keep.tile([P, SLOTS, PACK], BF16, name="tokg0", align_bytes=64)
-        tokg1 = [keep.tile([P, HALF, PACK], BF16, name="tokg1_%d" % h, align_bytes=64) for h in range(2)]
-        tok_codes = [keep.tile([P, SLOTS], U32, name="tok_codes%d" % g, align_bytes=64) for g in range(PASSES)]
+        tokg1 = keep.tile([P, SLOTS, PACK], BF16, name="tokg1", align_bytes=64)
+        tok_codes1 = keep.tile([P, SLOTS], U32, name="tok_codes1", align_bytes=64)
         tok_scales = [keep.tile([P, SLOTS], U8, name="tok_scales%d" % g, align_bytes=64) for g in range(PASSES)]
         w_grouped = [keep.tile([P, 4, N, PACK], BF16, name="w_grouped%d" % j, align_bytes=64) for j in range(4)]
         w_codes = keep.tile([P, 16 * N], U32, name="w_codes", align_bytes=64)
@@ -63,22 +63,13 @@ def tile_routed_moe_kernel(tc, xT, w, gate, offs, out):
         def gather(t, first, count):
             nc.vector.tensor_copy(g4[:, t, first : first + count], plane[1][t][:].indirect(listed(first, count)))
 
-        def interleave_tokens1(q):
-            src = g4[:, :, q * QUARTER : (q + 1) * QUARTER].rearrange("p t (c i) -> p c t i", i=4)
-            a = (q % 2) * QUARTER
-            dst = tokg1[q // 2][:, a : a + QUARTER, :].rearrange("p (c i) t -> p c t i", i=4)
-            if q in TOKENS_ON_VECTOR:
+        def interleave_tokens1(h):
+            src = g4[:, :, h * HALF : (h + 1) * HALF].rearrange("p t (c i) -> p c t i", i=4)
+            dst = tokg1[:, h * HALF : (h + 1) * HALF, :].rearrange("p (c i) t -> p c t i", i=4)
+            if h in TOKENS_ON_VECTOR:
                 nc.vector.tensor_copy(dst, src)
             else:
                 nc.scalar.copy(dst, src)
-
-        def quantize_tokens1(h):
-            cols = slice(h * HALF, (h + 1) * HALF)
-            nc.vector.quantize_mx(
-                out=tok_codes[1][:, cols].bitcast(FP8X4),
-                scales=tok_scales[1][:, cols],
-                in_=tokg1[h][:].rearrange("p n t -> p (n t)"),
-            )
 
         def interleave_expert(e):
             j, c = e // 2, 2 * (e % 2)
@@ -106,16 +97,21 @@ def tile_routed_moe_kernel(tc, xT, w, gate, offs, out):
             else:
                 for h in range(2):
                     gather(t, h * HALF, HALF)
-        for q in range(4):
-            interleave_tokens1(q)
+        for h in range(2):
+            interleave_tokens1(h)
 
+        tok_codes0 = keep.tile([P, SLOTS], U32, name="tok_codes0", tag="plane1_3", align_bytes=64)
+        tok_codes = [tok_codes0, tok_codes1]
         nc.vector.quantize_mx(
             out=tok_codes[0][:].bitcast(FP8X4),
             scales=tok_scales[0][:],
             in_=tokg0[:].rearrange("p n t -> p (n t)"),
         )
-        for h in range(2):
-            quantize_tokens1(h)
+        nc.vector.quantize_mx(
+            out=tok_codes[1][:].bitcast(FP8X4),
+            scales=tok_scales[1][:],
+            in_=tokg1[:].rearrange("p n t -> p (n t)"),
+        )
 
         sums = []
         acc = [psum.tile([P, C], F32, name="acc%d" % e) for e in range(E)]

@@ -152,4 +152,5 @@ def tile_routed_moe_kernel(tc, xT, w, gate, offs, out):
                 MULT,
             )
 
-        nc.sync.dma_start(out, window[:])
+        nc.sync.dma_start(out[:, 0 : T // 2], window[:, 0 : T // 2])
+        nc.scalar.dma_start(out[:, T // 2 : T], window[:, T // 2 : T])

@@ -48,7 +48,7 @@ def tile_routed_moe_kernel(tc, xT, w, gate, offs, out):
         nc.vector.memset(window[:], 0.0)
 
         plane16 = [keep.tile([P, T], BF16, name="plane16_%d" % t) for t in range(PACK)]
-        g4 = keep.tile([P, PACK, SLOTS], F32, name="g4")
+        pairs1 = keep.tile([P, 2, SLOTS, 2], BF16, name="pairs1", align_bytes=64)
         tokg0 = keep.tile([P, SLOTS, PACK], BF16, name="tokg0", align_bytes=64)
         tokg1 = keep.tile([P, SLOTS, PACK], BF16, name="tokg1", align_bytes=64)
         tok_codes1 = keep.tile([P, SLOTS], U32, name="tok_codes1", align_bytes=64)
@@ -61,11 +61,11 @@ def tile_routed_moe_kernel(tc, xT, w, gate, offs, out):
             return offs_sb[:, first // 16 : (first + count) // 16]
 
         def gather(t, first, count):
-            nc.vector.tensor_copy(g4[:, t, first : first + count], plane[1][t][:].indirect(listed(first, count)))
+            nc.vector.tensor_copy(pairs1[:, t // 2, first : first + count, t % 2], plane[1][t][:].indirect(listed(first, count)))
 
         def interleave_tokens1(h):
-            src = g4[:, :, h * HALF : (h + 1) * HALF].rearrange("p t (c i) -> p c t i", i=4)
-            dst = tokg1[:, h * HALF : (h + 1) * HALF, :].rearrange("p (c i) t -> p c t i", i=4)
+            src = pairs1[:].rearrange("p u s e -> p u (s e)").bitcast(F32)[:, :, h * HALF : (h + 1) * HALF].rearrange("p u s -> p s u")
+            dst = tokg1[:, h * HALF : (h + 1) * HALF, :].rearrange("p s t -> p (s t)").bitcast(F32).rearrange("p (s u) -> p s u", u=2)
             if h in TOKENS_ON_VECTOR:
                 nc.vector.tensor_copy(dst, src)
             else:

@@ -22,6 +22,7 @@ QUARTER = 256
 
 W_ON_VECTOR = (3,)
 TOKENS_ON_VECTOR = (1,)
+GATE_BEHIND = 2
 PLANE_ORDER = ((0, 0), (0, 1), (1, 0), (0, 2), (1, 1), (0, 3), (1, 2), (1, 3))
 
 
@@ -40,9 +41,10 @@ def tile_routed_moe_kernel(tc, xT, w, gate, offs, out):
 
         for g, t in PLANE_ORDER:
             nc.sync.dma_start(plane[g][t][:], planes_hbm[g, :, t, :])
-        nc.sync.dma_start(gate_sb[:], gate)
         for j in range(4):
             nc.sync.dma_start(w_raw[j][:], w_hbm[:, 4 * j : 4 * j + 4, :])
+            if j == GATE_BEHIND:
+                nc.sync.dma_start(gate_sb[:], gate)
 
         window = keep.tile([P, T], F32, name="window")
         nc.vector.memset(window[:], 0.0)
@@ -50,10 +52,10 @@ def tile_routed_moe_kernel(tc, xT, w, gate, offs, out):
         plane16 = [keep.tile([P, T], BF16, name="plane16_%d" % t) for t in range(PACK)]
         pairs1 = keep.tile([P, 2, SLOTS, 2], BF16, name="pairs1", align_bytes=64)
         tokg0 = keep.tile([P, SLOTS, PACK], BF16, name="tokg0", align_bytes=64)
-        tokg1 = keep.tile([P, SLOTS, PACK], BF16, name="tokg1", align_bytes=64)
-        tok_codes1 = keep.tile([P, SLOTS], U32, name="tok_codes1", align_bytes=64)
-        tok_scales = [keep.tile([P, SLOTS], U8, name="tok_scales%d" % g, align_bytes=64) for g in range(PASSES)]
-        w_grouped = [keep.tile([P, 4, N, PACK], BF16, name="w_grouped%d" % j, align_bytes=64) for j in range(4)]
+        tok_codes1 = [keep.tile([P, HALF], U32, name="tok_codes1_%d" % h, align_bytes=64) for h in range(2)]
+        tok_scales0 = keep.tile([P, SLOTS], U8, name="tok_scales0", align_bytes=64)
+        tok_scales1 = [keep.tile([P, HALF], U8, name="tok_scales1_%d" % h, align_bytes=64) for h in range(2)]
+        w_grouped = [keep.tile([P, 4, N, PACK], BF16, name="w_grouped%d" % j, tag="w_grouped%d" % j, align_bytes=64) for j in range(4)]
         w_codes = keep.tile([P, 16 * N], U32, name="w_codes", align_bytes=64)
         w_scales = keep.tile([P, 16 * N], U8, name="w_scales", align_bytes=64)
 
@@ -63,13 +65,19 @@ def tile_routed_moe_kernel(tc, xT, w, gate, offs, out):
         def gather(t, first, count):
             nc.vector.tensor_copy(pairs1[:, t // 2, first : first + count, t % 2], plane[1][t][:].indirect(listed(first, count)))
 
-        def interleave_tokens1(h):
+        def tokens1(h, tag):
+            tokg1 = keep.tile([P, HALF, PACK], BF16, name="tokg1_%d" % h, tag=tag, align_bytes=64)
             src = pairs1[:].rearrange("p u s e -> p u (s e)").bitcast(F32)[:, :, h * HALF : (h + 1) * HALF].rearrange("p u s -> p s u")
-            dst = tokg1[:, h * HALF : (h + 1) * HALF, :].rearrange("p s t -> p (s t)").bitcast(F32).rearrange("p (s u) -> p s u", u=2)
+            dst = tokg1[:].rearrange("p s t -> p (s t)").bitcast(F32).rearrange("p (s u) -> p s u", u=2)
             if h in TOKENS_ON_VECTOR:
                 nc.vector.tensor_copy(dst, src)
             else:
                 nc.scalar.copy(dst, src)
+            nc.vector.quantize_mx(
+                out=tok_codes1[h][:].bitcast(FP8X4),
+                scales=tok_scales1[h][:],
+                in_=tokg1[:].rearrange("p n t -> p (n t)"),
+            )
 
         def interleave_expert(e):
             j, c = e // 2, 2 * (e % 2)
@@ -97,34 +105,32 @@ def tile_routed_moe_kernel(tc, xT, w, gate, offs, out):
             else:
                 for h in range(2):
                     gather(t, h * HALF, HALF)
-        for h in range(2):
-            interleave_tokens1(h)
 
         tok_codes0 = keep.tile([P, SLOTS], U32, name="tok_codes0", tag="plane1_3", align_bytes=64)
-        tok_codes = [tok_codes0, tok_codes1]
         nc.vector.quantize_mx(
-            out=tok_codes[0][:].bitcast(FP8X4),
-            scales=tok_scales[0][:],
+            out=tok_codes0[:].bitcast(FP8X4),
+            scales=tok_scales0[:],
             in_=tokg0[:].rearrange("p n t -> p (n t)"),
         )
-        nc.vector.quantize_mx(
-            out=tok_codes[1][:].bitcast(FP8X4),
-            scales=tok_scales[1][:],
-            in_=tokg1[:].rearrange("p n t -> p (n t)"),
-        )
+        tokens1(0, "tokg1_0")
 
         sums = []
         acc = [psum.tile([P, C], F32, name="acc%d" % e) for e in range(E)]
 
         def multiply(e, g):
             wc = slice((2 * e + g) * N, (2 * e + g + 1) * N)
-            sc = slice(e * C, (e + 1) * C)
+            if g == 0:
+                sc = slice(e * C, (e + 1) * C)
+                codes, scales = tok_codes0, tok_scales0
+            else:
+                sc = slice((e % 4) * C, (e % 4 + 1) * C)
+                codes, scales = tok_codes1[e // 4], tok_scales1[e // 4]
             nc.tensor.matmul_mx(
                 out=acc[e][:],
                 lhsT=w_codes[:, wc].bitcast(FP8X4),
                 lhsT_scale=w_scales[:, wc],
-                rhs=tok_codes[g][:, sc].bitcast(FP8X4),
-                rhs_scale=tok_scales[g][:, sc],
+                rhs=codes[:, sc].bitcast(FP8X4),
+                rhs_scale=scales[:, sc],
                 start=(g == 0),
                 stop=(g == PASSES - 1),
             )
@@ -136,6 +142,8 @@ def tile_routed_moe_kernel(tc, xT, w, gate, offs, out):
                 interleave_expert(2 * j + 2)
                 interleave_expert(2 * j + 3)
             quantize_w(j)
+            if j == 0:
+                tokens1(1, "w_grouped0")
             multiply(2 * j, 0)
             multiply(2 * j + 1, 0)
             sums.append(keep.tile([P, 2 * C], F32, name="sums%d" % j, tag=("w_raw%d" % (j + 1)) if j < 3 else "sums3"))

@@ -33,18 +33,20 @@ def tile_routed_moe_kernel(tc, xT, w, gate, offs, out):
 
     with tc.tile_pool(name="keep", bufs=1) as keep, tc.psum_pool(name="psum", bufs=1) as psum:
         offs_sb = keep.tile([P, SLOTS // 16], U16, name="offs_sb")
-        nc.sync.dma_start(offs_sb[:], offs)
 
         plane = [[keep.tile([P, T], F32, name="plane%d_%d" % (g, t), tag="plane%d_%d" % (g, t), align_bytes=64) for t in range(PACK)] for g in range(PASSES)]
         w_raw = [keep.tile([P, 4, PACK * N], F32, name="w_raw%d" % j, tag="w_raw%d" % j) for j in range(4)]
-        gate_sb = keep.tile([P, SLOTS], F32, name="gate_sb")
+        gate_sb = [keep.tile([P, HALF], F32, name="gate_sb%d" % h) for h in range(2)]
 
         for g, t in PLANE_ORDER:
             nc.sync.dma_start(plane[g][t][:], planes_hbm[g, :, t, :])
+            if (g, t) == PLANE_ORDER[0]:
+                nc.sync.dma_start(offs_sb[:], offs)
         for j in range(4):
             nc.sync.dma_start(w_raw[j][:], w_hbm[:, 4 * j : 4 * j + 4, :])
-            if j == GATE_BEHIND:
-                nc.sync.dma_start(gate_sb[:], gate)
+            if j >= GATE_BEHIND:
+                h = j - GATE_BEHIND
+                nc.sync.dma_start(gate_sb[h][:], gate[:, h * HALF : (h + 1) * HALF])
 
         window = keep.tile([P, T], F32, name="window")
         nc.vector.memset(window[:], 0.0)
@@ -144,10 +146,9 @@ def tile_routed_moe_kernel(tc, xT, w, gate, offs, out):
             quantize_w(j)
             if j == 0:
                 tokens1(1, "w_grouped0")
-            multiply(2 * j, 0)
-            multiply(2 * j + 1, 0)
             sums.append(keep.tile([P, 2 * C], F32, name="sums%d" % j, tag=("w_raw%d" % (j + 1)) if j < 3 else "sums3"))
             for e in (2 * j, 2 * j + 1):
+                multiply(e, 0)
                 multiply(e, 1)
                 nc.scalar.copy(sums[j][:, (e % 2) * C : (e % 2 + 1) * C], acc[e][:])
 
@@ -156,7 +157,7 @@ def tile_routed_moe_kernel(tc, xT, w, gate, offs, out):
             nc.vector.tensor_tensor(
                 window[:].indirect(listed(first, QUARTER)),
                 sums[j][:],
-                gate_sb[:, first : first + QUARTER],
+                gate_sb[j // 2][:, (j % 2) * QUARTER : (j % 2 + 1) * QUARTER],
                 MULT,
             )
 

import concourse.mybir as mybir

FLOPS = 2 * 1024 * 128 * 1024

K, T, E, C, N = 1024, 2048, 8, 128, 128
P = 128
PACK = 4
PASSES = K // (P * PACK)
SLOTS = E * C

F32 = mybir.dt.float32
BF16 = mybir.dt.bfloat16
U32 = mybir.dt.uint32
U16 = mybir.dt.uint16
U8 = mybir.dt.uint8
FP8X4 = mybir.dt.float8_e4m3fn_x4
MULT = mybir.AluOpType.mult
COPY = mybir.ActivationFunctionType.Copy

HALF = 512
QUARTER = 256

W_ON_VECTOR = (3,)
TOKENS_ON_VECTOR = (1,)
GATE_BEHIND = 2
PLANE_ORDER = ((0, 0), (0, 1), (1, 0), (0, 2), (1, 1), (0, 3), (1, 2), (1, 3))


def tile_routed_moe_kernel(tc, xT, w, gate, offs, out):
    nc = tc.nc
    planes_hbm = xT.rearrange("(g p t) n -> g p t n", p=P, t=PACK)
    w_hbm = w.flatten_outer_dims().rearrange("(c p t) n -> p c (t n)", p=P, t=PACK)

    with tc.tile_pool(name="keep", bufs=1) as keep, tc.psum_pool(name="psum", bufs=1) as psum:
        offs_sb = keep.tile([P, SLOTS // 16], U16, name="offs_sb")

        plane = [[keep.tile([P, T], F32, name="plane%d_%d" % (g, t), tag="plane%d_%d" % (g, t), align_bytes=64) for t in range(PACK)] for g in range(PASSES)]
        w_raw = [keep.tile([P, 4, PACK * N], F32, name="w_raw%d" % j, tag="w_raw%d" % j) for j in range(4)]
        gate_sb = [keep.tile([P, HALF], F32, name="gate_sb%d" % h) for h in range(2)]

        for g, t in PLANE_ORDER:
            nc.sync.dma_start(plane[g][t][:], planes_hbm[g, :, t, :])
            if (g, t) == PLANE_ORDER[0]:
                nc.sync.dma_start(offs_sb[:], offs)
        for j in range(4):
            nc.sync.dma_start(w_raw[j][:], w_hbm[:, 4 * j : 4 * j + 4, :])
            if j >= GATE_BEHIND:
                h = j - GATE_BEHIND
                nc.sync.dma_start(gate_sb[h][:], gate[:, h * HALF : (h + 1) * HALF])

        window = keep.tile([P, T], F32, name="window")
        nc.vector.memset(window[:], 0.0)

        plane16 = [keep.tile([P, T], BF16, name="plane16_%d" % t) for t in range(PACK)]
        pairs1 = keep.tile([P, 2, SLOTS, 2], BF16, name="pairs1", align_bytes=64)
        tokg0 = keep.tile([P, SLOTS, PACK], BF16, name="tokg0", align_bytes=64)
        tok_codes1 = [keep.tile([P, HALF], U32, name="tok_codes1_%d" % h, align_bytes=64) for h in range(2)]
        tok_scales0 = keep.tile([P, SLOTS], U8, name="tok_scales0", align_bytes=64)
        tok_scales1 = [keep.tile([P, HALF], U8, name="tok_scales1_%d" % h, align_bytes=64) for h in range(2)]
        w_grouped = [keep.tile([P, 4, N, PACK], BF16, name="w_grouped%d" % j, tag="w_grouped%d" % j, align_bytes=64) for j in range(4)]
        w_codes = keep.tile([P, 16 * N], U32, name="w_codes", align_bytes=64)
        w_scales = keep.tile([P, 16 * N], U8, name="w_scales", align_bytes=64)

        def listed(first, count):
            return offs_sb[:, first // 16 : (first + count) // 16]

        def gather(t, first, count):
            nc.vector.tensor_copy(pairs1[:, t // 2, first : first + count, t % 2], plane[1][t][:].indirect(listed(first, count)))

        def tokens1(h, tag):
            tokg1 = keep.tile([P, HALF, PACK], BF16, name="tokg1_%d" % h, tag=tag, align_bytes=64)
            src = pairs1[:].rearrange("p u s e -> p u (s e)").bitcast(F32)[:, :, h * HALF : (h + 1) * HALF].rearrange("p u s -> p s u")
            dst = tokg1[:].rearrange("p s t -> p (s t)").bitcast(F32).rearrange("p (s u) -> p s u", u=2)
            if h in TOKENS_ON_VECTOR:
                nc.vector.tensor_copy(dst, src)
            else:
                nc.scalar.copy(dst, src)
            nc.vector.quantize_mx(
                out=tok_codes1[h][:].bitcast(FP8X4),
                scales=tok_scales1[h][:],
                in_=tokg1[:].rearrange("p n t -> p (n t)"),
            )

        def interleave_expert(e):
            j, c = e // 2, 2 * (e % 2)
            dst = w_grouped[j][:, c : c + 2, :, :].rearrange("p c (b i) t -> p c b t i", i=4)
            src = w_raw[j][:, c : c + 2, :].rearrange("p c (t b i) -> p c b t i", t=PACK, i=4)
            if e in W_ON_VECTOR:
                nc.vector.tensor_copy(dst, src)
            else:
                nc.scalar.copy(dst, src)

        def quantize_w(j):
            cols = slice(j * 4 * N, (j + 1) * 4 * N)
            nc.vector.quantize_mx(
                out=w_codes[:, cols].bitcast(FP8X4),
                scales=w_scales[:, cols],
                in_=w_grouped[j][:].rearrange("p c n t -> p (c n t)"),
            )

        for g, t in PLANE_ORDER:
            if g == 0:
                nc.vector.tensor_copy(plane16[t][:], plane[0][t][:])
                nc.scalar.activation(tokg0[:, :, t], plane16[t][:].indirect(listed(0, SLOTS)), COPY)
            elif t < PACK - 1:
                gather(t, 0, SLOTS)
            else:
                for h in range(2):
                    gather(t, h * HALF, HALF)

        tok_codes0 = keep.tile([P, SLOTS], U32, name="tok_codes0", tag="plane1_3", align_bytes=64)
        nc.vector.quantize_mx(
            out=tok_codes0[:].bitcast(FP8X4),
            scales=tok_scales0[:],
            in_=tokg0[:].rearrange("p n t -> p (n t)"),
        )
        tokens1(0, "tokg1_0")

        sums = []
        acc = [psum.tile([P, C], F32, name="acc%d" % e) for e in range(E)]

        def multiply(e, g):
            wc = slice((2 * e + g) * N, (2 * e + g + 1) * N)
            if g == 0:
                sc = slice(e * C, (e + 1) * C)
                codes, scales = tok_codes0, tok_scales0
            else:
                sc = slice((e % 4) * C, (e % 4 + 1) * C)
                codes, scales = tok_codes1[e // 4], tok_scales1[e // 4]
            nc.tensor.matmul_mx(
                out=acc[e][:],
                lhsT=w_codes[:, wc].bitcast(FP8X4),
                lhsT_scale=w_scales[:, wc],
                rhs=codes[:, sc].bitcast(FP8X4),
                rhs_scale=scales[:, sc],
                start=(g == 0),
                stop=(g == PASSES - 1),
            )

        interleave_expert(0)
        interleave_expert(1)
        for j in range(4):
            if j < 3:
                interleave_expert(2 * j + 2)
                interleave_expert(2 * j + 3)
            quantize_w(j)
            if j == 0:
                tokens1(1, "w_grouped0")
            sums.append(keep.tile([P, 2 * C], F32, name="sums%d" % j, tag=("w_raw%d" % (j + 1)) if j < 3 else "sums3"))
            for e in (2 * j, 2 * j + 1):
                multiply(e, 0)
                multiply(e, 1)
                nc.scalar.copy(sums[j][:, (e % 2) * C : (e % 2 + 1) * C], acc[e][:])

        for j in range(4):
            first = j * QUARTER
            nc.vector.tensor_tensor(
                window[:].indirect(listed(first, QUARTER)),
                sums[j][:],
                gate_sb[j // 2][:, (j % 2) * QUARTER : (j % 2 + 1) * QUARTER],
                MULT,
            )

        nc.sync.dma_start(out[:, 0 : T // 2], window[:, 0 : T // 2])
        nc.scalar.dma_start(out[:, T // 2 : T], window[:, T // 2 : T])
